import numpy as np
import ml_dtypes


def mxq(x, axis, fmt="e4m3"):
    dtype, down = {"e4m3": (ml_dtypes.float8_e4m3fn, 7), "e5m2": (ml_dtypes.float8_e5m2, 14)}[fmt]
    v = np.moveaxis(np.asarray(x, np.float32).astype(ml_dtypes.bfloat16).astype(np.float64), axis, -1)
    blocks = v.reshape(v.shape[:-1] + (-1, 32))
    amax = np.abs(blocks).max(-1, keepdims=True)
    byte = np.maximum(np.where(amax > 0, np.frexp(amax)[1] - 1 + 127, 0) - down, 1)
    scale = np.exp2(byte - 127.0)
    codes = (blocks / scale).astype(np.float32).astype(dtype).astype(np.float64)
    return np.moveaxis((codes * scale).reshape(v.shape), -1, axis)


WIDE = False


def mx_kscale(k):
    if not WIDE:
        return np.ones(k)
    levels = np.array([10, -10, 5, -5, 0])
    if k % 512:
        return np.exp2(np.random.permutation(np.resize(levels, k // 32))).repeat(32)
    a = np.empty((k // 512, 16))
    for p in range(k // 512):
        a[p, :8] = np.random.permutation(np.resize(levels, 8))
        for g in range(8):
            far = levels[np.abs(levels - a[p, g]) >= 10]
            a[p, g + 8] = far[np.random.randint(len(far))]
    return np.exp2(a.ravel()).repeat(32)


def f64(x):
    return np.asarray(x).astype(np.float64)


def striped(idx):
    return np.tile(idx.reshape(-1, 16).T, (8, 1)).astype(np.uint16)


def unstriped(offs):
    return offs[:16].T.reshape(-1).astype(np.int64)


def pack_weight(w):
    k, n = w.shape
    w = f64(np.asarray(w, np.float32).astype(ml_dtypes.bfloat16)).reshape(k // 32, 32, n)
    amax = np.abs(w).max(1)
    byte = np.clip(np.where(amax > 0, np.frexp(amax)[1] - 1 + 127 - 7, 1), 1, 254)
    scaled = (w * np.exp2(127.0 - byte)[:, None, :]).reshape(k, n).astype(np.float32)
    words = np.ascontiguousarray(scaled.reshape(k // 512, 128, 4, n).transpose(0, 1, 3, 2)).astype(ml_dtypes.float8_e4m3fn).view(np.uint8)
    return words, np.ascontiguousarray(byte.astype(np.uint8).reshape(k // 512, 16, n))


def unpack_weight(words, scales):
    g, p, n, _ = words.shape
    vals = np.ascontiguousarray(words).view(ml_dtypes.float8_e4m3fn).astype(np.float64) * np.repeat(np.exp2(scales.astype(np.float64) - 127.0), 8, axis=1)[..., None]
    return vals.transpose(0, 1, 3, 2).reshape(g * 512, n)


def relu(v):
    return np.maximum(v, 0.0)


K, T, S, N, H = 512, 2048, 512, 128, 512


def setup_inputs():
    n = np.random.standard_normal
    s = mx_kscale(K)[:, None]
    u = mx_kscale(H)
    packed_xT = pack_weight(n((K, T)) * s)
    return {
        "x_words": packed_xT[0],
        "x_scales": packed_xT[1],
        "w1": (n((K, H)) / np.sqrt(K) / s).astype(np.float32),
        "w2": (n((K, H)) / np.sqrt(K) / s).astype(np.float32),
        "slack": (np.random.uniform(0.2, 2.0, (H, S))).astype(np.float32),
        "unit": (np.random.uniform(0.6, 1.4, (H, 1)) * u[:, None]).astype(np.float32),
        "w3": (n((H, N)) / np.sqrt(H) / u[:, None]).astype(np.float32),
        "offs": striped(np.random.permutation(T)[:S]),
        "pre": striped(np.random.permutation(S)),
        "suc": striped(np.random.permutation(S)),
        "req": striped(np.random.permutation(S)),
    }


def reference(x_words, x_scales, w1, w2, slack, unit, w3, offs, pre, suc, req):
    xq = unpack_weight(x_words, x_scales)[:, unstriped(offs)]
    px = mxq(f64(w1), 0, "e4m3").T @ xq
    dx1 = np.abs(px[:, unstriped(pre)] - px[:, unstriped(req)])
    py = mxq(f64(w2), 0, "e4m3").T @ xq
    dy1 = np.abs(py[:, unstriped(pre)] - py[:, unstriped(req)])
    dx2 = np.abs(px[:, unstriped(req)] - px[:, unstriped(suc)])
    dy2 = np.abs(py[:, unstriped(req)] - py[:, unstriped(suc)])
    dx3 = np.abs(px[:, unstriped(pre)] - px[:, unstriped(suc)])
    ins = dx1 + dy1 + dx2 + dy2 - dx3
    late = relu(0.5 * ins - f64(slack))
    hid = f64(unit) * (ins + 1.5 * late)
    return mxq(f64(w3), 0, "e4m3").T @ mxq(hid, 0, "e4m3")

@@ -1,0 +1,205 @@
+from contextlib import ExitStack
+
+import concourse.mybir as mybir
+from concourse.masks import make_identity
+
+K, T, S, N, H = 512, 2048, 512, 128, 512
+FLOPS = 2 * K * H * S * 2 + 2 * H * N * S
+
+F32 = mybir.dt.float32
+BF16 = mybir.dt.bfloat16
+I32 = mybir.dt.int32
+U32 = mybir.dt.uint32
+U16 = mybir.dt.uint16
+U8 = mybir.dt.uint8
+FP8X4 = mybir.dt.float8_e4m3fn_x4
+ALU = mybir.AluOpType
+ACT = mybir.ActivationFunctionType
+
+P = 128
+ROWS = H // P
+SPARE = 16
+GROUPS = ((0, 256), (256, 128), (384, 128))
+
+
+def tile_picked_ydarpi_cost_p_kernel(tc, x_words, x_scales, w1, w2, slack, unit, w3, offs, pre, suc, req, out):
+    nc = tc.nc
+    with ExitStack() as ctx:
+        keep = ctx.enter_context(tc.tile_pool(name="keep", bufs=1))
+        work = ctx.enter_context(tc.tile_pool(name="work", bufs=3))
+        psum = ctx.enter_context(tc.psum_pool(name="psum", bufs=2))
+        psum1 = ctx.enter_context(tc.psum_pool(name="psum1", bufs=1))
+
+        l_offs = keep.tile([P, S // 16], U16, name="l_offs")
+        l_pre = keep.tile([P, S // 16], U16, name="l_pre")
+        l_suc = keep.tile([P, S // 16], U16, name="l_suc")
+        l_req = keep.tile([P, S // 16], U16, name="l_req")
+        xw = keep.tile([P, T], I32, name="xw")
+        xs = keep.tile([P, T], U8, name="xs")
+        un = keep.tile([P, ROWS], F32, name="un")
+        un4 = keep.tile([P, 4], F32, name="un4")
+        w_raw = [[keep.tile([P, 4, P], F32, name="wraw%d_%d" % (a, r)) for r in range(ROWS)] for a in range(2)]
+        w3_raw = keep.tile([P, 4, N], F32, name="w3_raw")
+        sl = [keep.tile([P, S], F32, name="sl%d" % r) for r in range(ROWS)]
+        pos = [[keep.tile([P, S + SPARE], F32, name="pos%d_%d" % (a, r)) for r in range(ROWS)] for a in range(2)]
+        ident = keep.tile([P, P], F32, name="ident")
+
+        for q in range(4):
+            nc.scalar.dma_start(out=xs[32 * q:32 * q + 32, :].bitcast(I32),
+                                in_=x_scales[0, 4 * q:4 * q + 4, :].bitcast(I32).partition_broadcast(8))
+        ws = [w.rearrange("(p j) c -> p j c", j=4) for w in (w1, w2)]
+
+        def load_w(a, r):
+            nc.sync.dma_start(out=w_raw[a][r][:], in_=ws[a][:, :, r * P:(r + 1) * P])
+
+        nc.sync.dma_start(l_offs[:], offs)
+        nc.sync.dma_start(out=xw[:], in_=x_words[0].rearrange("p n t -> p (n t)").bitcast(I32))
+        load_w(0, 0)
+        with nc.allow_non_contiguous_dma(reason="one value a partition"):
+            nc.sync.dma_start(out=un[:], in_=unit.rearrange("(r p) o -> p (r o)", p=P))
+        nc.sync.dma_start(l_req[:], req)
+        load_w(1, 0)
+        nc.sync.dma_start(l_pre[:], pre)
+        nc.sync.dma_start(l_suc[:], suc)
+        for r in range(1, ROWS):
+            load_w(0, r)
+            load_w(1, r)
+            nc.sync.dma_start(out=sl[r - 1][:], in_=slack[(r - 1) * P:r * P, :])
+        nc.sync.dma_start(out=sl[ROWS - 1][:], in_=slack[(ROWS - 1) * P:, :])
+        nc.sync.dma_start(out=w3_raw[:], in_=w3.rearrange("(p j) n -> p j n", j=4))
+        nc.sync.dma_start(out=un4[:], in_=unit.rearrange("(p j) o -> p (j o)", j=4))
+
+        make_identity(nc, ident[:])
+        for a in range(2):
+            for r in range(ROWS):
+                nc.gpsimd.memset(pos[a][r][:, S:], 0.0)
+
+        mag = keep.tile([P, ROWS], F32, name="mag")
+        half_mag = keep.tile([P, ROWS], F32, name="half_mag")
+        neg_mag = keep.tile([P, ROWS], F32, name="neg_mag")
+        nc.scalar.activation(out=mag[:], in_=un[:], func=ACT.Abs)
+        nc.scalar.activation(out=half_mag[:], in_=un[:], func=ACT.Abs, scale=0.5)
+        nc.scalar.activation(out=neg_mag[:], in_=mag[:], func=ACT.Copy, scale=-1.0)
+
+        gs = keep.tile([P, S], U8, name="gs", align_bytes=64)
+        gw = keep.tile([P, S], U32, name="gw", align_bytes=64)
+        nc.vector.tensor_copy(gs[:], xs[:].indirect(l_offs[:]))
+        nc.vector.tensor_copy(gw[:], xw[:].bitcast(U32).indirect(l_offs[:]))
+
+        def position(a, r):
+            raw = w_raw[a][r][:]
+            cast = nc.scalar.copy if r in (0,) else nc.vector.tensor_copy
+            wg = work.tile([P, P, 4], BF16, name="wg", align_bytes=64, bufs=4)
+            cast(out=wg[:].rearrange("p (c i) j -> p c j i", i=4), in_=raw.rearrange("p j (c i) -> p c j i", i=4))
+            wc = work.tile([P, P], U32, name="wc", align_bytes=64, bufs=4)
+            wsc = work.tile([P, P], U8, name="wsc", align_bytes=64, bufs=4)
+            nc.vector.quantize_mx(out=wc[:].bitcast(FP8X4), scales=wsc[:], in_=wg[:].rearrange("p c j -> p (c j)"))
+            acc = psum.tile([P, S], F32, name="acc")
+            nc.tensor.matmul_mx(out=acc[:], lhsT=wc[:].bitcast(FP8X4), lhsT_scale=wsc[:], rhs=gw[:].bitcast(FP8X4), rhs_scale=gs[:], start=True, stop=True)
+            factor = (mag, half_mag)[a][:, r:r + 1]
+            if (a, r) == (1, 0):
+                nc.vector.tensor_scalar(out=pos[a][r][:, :S], in0=acc[:], scalar1=factor, scalar2=None, op0=ALU.mult)
+            else:
+                nc.scalar.activation(out=pos[a][r][:, :S], in_=acc[:], func=ACT.Copy, scale=factor)
+
+        hid_t = [keep.tile([P, n // P, H], BF16, name="hid_t%d" % j0) for j0, n in GROUPS]
+
+        def add_turned(bank, term, n, first, last):
+            for c in range(n // P):
+                nc.tensor.matmul(bank[:, c * P:(c + 1) * P], lhsT=term[:, c * P:(c + 1) * P], rhs=ident[:], is_transpose=True,
+                                 start=first and c == 0, stop=last and c == n // P - 1)
+
+        def fetch_req(r, j0, n):
+            cols = slice(j0 // 16, (j0 + n) // 16)
+            nb = work.tile([P, n], F32, name="nb", bufs=3)
+            ne = work.tile([P, n], F32, name="ne", bufs=3)
+            nc.scalar.activation(out=nb[:], in_=pos[0][r][:].indirect(l_req[:, cols]), func=ACT.Copy, scale=-1.0)
+            nc.scalar.activation(out=ne[:], in_=pos[1][r][:].indirect(l_req[:, cols]), func=ACT.Copy, scale=-1.0)
+            return nb[:], ne[:]
+
+        def costs(r, j0, n, nb, ne):
+            cols = slice(j0 // 16, (j0 + n) // 16)
+            px, py = pos[0][r], pos[1][r]
+
+            def fresh(tag):
+                return work.tile([P, n], F32, name=tag)
+
+            ns = fresh("ns")
+            nc.scalar.activation(out=ns[:], in_=sl[r][:, j0:j0 + n], func=ACT.Copy, scale=neg_mag[:, r:r + 1])
+            u, w, p, q, t, med = fresh("u"), fresh("w"), fresh("p"), fresh("q"), fresh("t"), fresh("med")
+            nc.vector.tensor_tensor(u[:], px[:].indirect(l_pre[:, cols]), nb, ALU.add)
+            nc.vector.tensor_tensor(w[:], px[:].indirect(l_suc[:, cols]), nb, ALU.add)
+            nc.vector.tensor_tensor(p[:], py[:].indirect(l_pre[:, cols]), ne, ALU.add)
+            nc.vector.scalar_tensor_tensor(out=t[:], in0=u[:], scalar=0.0, in1=w[:], op0=ALU.min, op1=ALU.max)
+            nc.vector.tensor_tensor(q[:], py[:].indirect(l_suc[:, cols]), ne, ALU.add)
+            nc.vector.scalar_tensor_tensor(out=med[:], in0=u[:], scalar=0.0, in1=t[:], op0=ALU.max, op1=ALU.min)
+            ap, aq, am = fresh("ap"), fresh("aq"), fresh("am")
+            nc.scalar.activation(out=ap[:], in_=p[:], func=ACT.Abs)
+            nc.scalar.activation(out=aq[:], in_=q[:], func=ACT.Abs)
+            nc.scalar.activation(out=am[:], in_=med[:], func=ACT.Abs)
+            over = psum.tile([P, n], F32, name="over")
+            half = psum.tile([P, n], F32, name="half")
+            add_turned(over, ns, n, True, False)
+            add_turned(over, ap, n, False, False)
+            add_turned(half, ap, n, True, False)
+            add_turned(over, aq, n, False, False)
+            add_turned(half, aq, n, False, False)
+            add_turned(over, am, n, False, True)
+            add_turned(half, am, n, False, True)
+            late = u
+            nc.scalar.activation(out=late[:], in_=over[:], func=ACT.Relu, scale=1.5)
+            for g, (g0, gn) in enumerate(GROUPS):
+                if j0 <= g0 < j0 + n:
+                    part = slice(g0 - j0, g0 - j0 + gn)
+                    nc.vector.scalar_tensor_tensor(
+                        out=hid_t[g][:, :, r * P:(r + 1) * P],
+                        in0=half[:, part].rearrange("p (c i) -> p c i", i=P), scalar=2.0,
+                        in1=late[:, part].rearrange("p (c i) -> p c i", i=P), op0=ALU.mult, op1=ALU.add)
+
+        w3c = keep.tile([P, N], U32, name="w3c", align_bytes=64)
+        w3s = keep.tile([P, N], U8, name="w3s", align_bytes=64)
+
+        def last_weights():
+            pos_unit = keep.tile([P, 4], F32, name="pos_unit")
+            sign = keep.tile([P, 4], F32, name="sign")
+            nc.vector.tensor_scalar(out=pos_unit[:], in0=un4[:], scalar1=0.0, scalar2=2.0, op0=ALU.is_ge, op1=ALU.mult)
+            nc.vector.tensor_scalar(out=sign[:], in0=pos_unit[:], scalar1=-1.0, scalar2=None, op0=ALU.add)
+            w3g = keep.tile([P, N, 4], BF16, name="w3g", align_bytes=64)
+            nc.vector.tensor_tensor(w3g[:], w3_raw[:].rearrange("p j n -> p n j"), sign[:].unsqueeze(1).to_broadcast([P, N, 4]), ALU.mult)
+            nc.vector.quantize_mx(out=w3c[:].bitcast(FP8X4), scales=w3s[:], in_=w3g[:].rearrange("p n j -> p (n j)"))
+
+        def vehicles(g):
+            j0, n = GROUPS[g]
+            words = hid_t[g][:].rearrange("p c i -> p (c i)").bitcast(F32)
+            back = psum1.tile([P, n // P, 2, P], F32, name="back")
+            for c in range(n // P):
+                for e in range(2):
+                    nc.tensor.transpose(back[:, c, e, :], words[:, c * 256 + e:(c + 1) * 256:2], ident[:])
+            hg = work.tile([P, n * 4], BF16, name="hg", align_bytes=64)
+            nc.scalar.copy(out=hg[:].bitcast(F32).rearrange("p (c j e) -> p c j e", j=P, e=2), in_=back[:].rearrange("p c e j -> p c j e"))
+            hc = work.tile([P, n], U32, name="hc", align_bytes=64)
+            hs = work.tile([P, n], U8, name="hs", align_bytes=64)
+            nc.vector.quantize_mx(out=hc[:].bitcast(FP8X4), scales=hs[:], in_=hg[:])
+            res = psum1.tile([P, n], F32, name="res")
+            nc.tensor.matmul_mx(out=res[:], lhsT=w3c[:].bitcast(FP8X4), lhsT_scale=w3s[:], rhs=hc[:].bitcast(FP8X4), rhs_scale=hs[:], start=True, stop=True)
+            res_sb = work.tile([P, n], F32, name="res_sb")
+            nc.scalar.copy(out=res_sb[:], in_=res[:])
+            nc.sync.dma_start(out=out[:, j0:j0 + n], in_=res_sb[:])
+
+        position(0, 0)
+        position(1, 0)
+        fetched = fetch_req(0, 0, S)
+        for r in range(1, ROWS):
+            position(0, r)
+            position(1, r)
+        for r in range(ROWS - 1):
+            ahead = fetch_req(r + 1, 0, S)
+            costs(r, 0, S, *fetched)
+            fetched = ahead
+            if r == 0:
+                last_weights()
+        for g, (j0, n) in enumerate(GROUPS):
+            costs(ROWS - 1, j0, n, *[f[:, j0:j0 + n] for f in fetched])
+            if g > 0:
+                vehicles(g - 1)
+        vehicles(len(GROUPS) - 1)

@@ -44,9 +44,9 @@ def tile_picked_ydarpi_cost_p_kernel(tc, x_words, x_scales, w1, w2, slack, unit,
         pos = [[keep.tile([P, S + SPARE], F32, name="pos%d_%d" % (a, r)) for r in range(ROWS)] for a in range(2)]
         ident = keep.tile([P, P], F32, name="ident")
 
+        nc.vector.memset(xs[:].bitcast(I32), 0)
         for q in range(4):
-            nc.scalar.dma_start(out=xs[32 * q:32 * q + 32, :].bitcast(I32),
-                                in_=x_scales[0, 4 * q:4 * q + 4, :].bitcast(I32).partition_broadcast(8))
+            nc.scalar.dma_start(out=xs[32 * q:32 * q + 4, :].bitcast(I32), in_=x_scales[0, 4 * q:4 * q + 4, :].bitcast(I32))
         ws = [w.rearrange("(p j) c -> p j c", j=4) for w in (w1, w2)]
 
         def load_w(a, r):
@@ -125,13 +125,23 @@ def tile_picked_ydarpi_cost_p_kernel(tc, x_words, x_scales, w1, w2, slack, unit,
                 return work.tile([P, n], F32, name=tag)
 
             ns = fresh("ns")
-            nc.scalar.activation(out=ns[:], in_=sl[r][:, j0:j0 + n], func=ACT.Copy, scale=neg_mag[:, r:r + 1])
+            nc.vector.tensor_scalar(out=ns[:], in0=sl[r][:, j0:j0 + n], scalar1=neg_mag[:, r:r + 1], scalar2=None, op0=ALU.mult)
             u, w, p, q, t, med = fresh("u"), fresh("w"), fresh("p"), fresh("q"), fresh("t"), fresh("med")
             nc.vector.tensor_tensor(u[:], px[:].indirect(l_pre[:, cols]), nb, ALU.add)
             nc.vector.tensor_tensor(w[:], px[:].indirect(l_suc[:, cols]), nb, ALU.add)
-            nc.vector.tensor_tensor(p[:], py[:].indirect(l_pre[:, cols]), ne, ALU.add)
+            if r in (3,):
+                d = fresh("d")
+                nc.scalar.activation(out=d[:], in_=py[:].indirect(l_pre[:, cols]), func=ACT.Copy)
+                nc.vector.tensor_tensor(p[:], d[:], ne, ALU.add)
+            else:
+                nc.vector.tensor_tensor(p[:], py[:].indirect(l_pre[:, cols]), ne, ALU.add)
             nc.vector.scalar_tensor_tensor(out=t[:], in0=u[:], scalar=0.0, in1=w[:], op0=ALU.min, op1=ALU.max)
-            nc.vector.tensor_tensor(q[:], py[:].indirect(l_suc[:, cols]), ne, ALU.add)
+            if r in (0, 1, 2, 3):
+                f = fresh("f")
+                nc.scalar.activation(out=f[:], in_=py[:].indirect(l_suc[:, cols]), func=ACT.Copy)
+                nc.vector.tensor_tensor(q[:], f[:], ne, ALU.add)
+            else:
+                nc.vector.tensor_tensor(q[:], py[:].indirect(l_suc[:, cols]), ne, ALU.add)
             nc.vector.scalar_tensor_tensor(out=med[:], in0=u[:], scalar=0.0, in1=t[:], op0=ALU.max, op1=ALU.min)
             ap, aq, am = fresh("ap"), fresh("aq"), fresh("am")
             nc.scalar.activation(out=ap[:], in_=p[:], func=ACT.Abs)
@@ -146,7 +156,7 @@ def tile_picked_ydarpi_cost_p_kernel(tc, x_words, x_scales, w1, w2, slack, unit,
             add_turned(half, aq, n, False, False)
             add_turned(over, am, n, False, True)
             add_turned(half, am, n, False, True)
-            late = u
+            late = fresh("late")
             nc.scalar.activation(out=late[:], in_=over[:], func=ACT.Relu, scale=1.5)
             for g, (g0, gn) in enumerate(GROUPS):
                 if j0 <= g0 < j0 + n:

@@ -4,7 +4,7 @@ import concourse.mybir as mybir
 from concourse.masks import make_identity
 
 K, T, S, N, H = 512, 2048, 512, 128, 512
-FLOPS = 2 * K * H * S * 2 + 2 * H * N * S
+FLOPS = 2 * (2 * K * H * S) + 2 * H * N * S
 
 F32 = mybir.dt.float32
 BF16 = mybir.dt.bfloat16
@@ -17,9 +17,17 @@ ALU = mybir.AluOpType
 ACT = mybir.ActivationFunctionType
 
 P = 128
-ROWS = H // P
+PACK = 4
+STRIPE = 16
+ROW_TILES = H // P
+LAST = ROW_TILES - 1
+X, Y = 0, 1
 SPARE = 16
-GROUPS = ((0, 256), (256, 128), (384, 128))
+PIECES = ((0, 256), (256, 128), (384, 128))
+SUC_ON_SCALAR_FROM = 2
+PRE_ON_SCALAR_FROM = 3
+SLACK_ON_SCALAR_FROM = 2
+AHEAD = 2
 
 
 def tile_picked_ydarpi_cost_p_kernel(tc, x_words, x_scales, w1, w2, slack, unit, w3, offs, pre, suc, req, out):
@@ -28,188 +36,204 @@ def tile_picked_ydarpi_cost_p_kernel(tc, x_words, x_scales, w1, w2, slack, unit,
         keep = ctx.enter_context(tc.tile_pool(name="keep", bufs=1))
         work = ctx.enter_context(tc.tile_pool(name="work", bufs=3))
         psum = ctx.enter_context(tc.psum_pool(name="psum", bufs=2))
-        psum1 = ctx.enter_context(tc.psum_pool(name="psum1", bufs=1))
+        psum_last = ctx.enter_context(tc.psum_pool(name="psum_last", bufs=1))
 
-        l_offs = keep.tile([P, S // 16], U16, name="l_offs")
-        l_pre = keep.tile([P, S // 16], U16, name="l_pre")
-        l_suc = keep.tile([P, S // 16], U16, name="l_suc")
-        l_req = keep.tile([P, S // 16], U16, name="l_req")
-        xw = keep.tile([P, T], I32, name="xw")
-        xs = keep.tile([P, T], U8, name="xs")
-        un = keep.tile([P, ROWS], F32, name="un")
-        un4 = keep.tile([P, 4], F32, name="un4")
-        w_raw = [[keep.tile([P, 4, P], F32, name="wraw%d_%d" % (a, r)) for r in range(ROWS)] for a in range(2)]
-        w3_raw = keep.tile([P, 4, N], F32, name="w3_raw")
-        sl = [keep.tile([P, S], F32, name="sl%d" % r) for r in range(ROWS)]
-        pos = [[keep.tile([P, S + SPARE], F32, name="pos%d_%d" % (a, r)) for r in range(ROWS)] for a in range(2)]
+        offs_list = keep.tile([P, S // STRIPE], U16, name="offs_list")
+        pre_list = keep.tile([P, S // STRIPE], U16, name="pre_list")
+        suc_list = keep.tile([P, S // STRIPE], U16, name="suc_list")
+        req_list = keep.tile([P, S // STRIPE], U16, name="req_list")
+        table_words = keep.tile([P, T], I32, name="table_words")
+        table_scales = keep.tile([P, T], U8, name="table_scales")
+        unit_by_tile = keep.tile([P, ROW_TILES], F32, name="unit_by_tile")
+        unit_by_word = [keep.tile([P, 2], F32, name="unit_by_word%d" % u) for u in range(2)]
+        w_raw = [[keep.tile([P, PACK, P], F32, name="w_raw%d_%d" % (c, r)) for r in range(ROW_TILES)] for c in (X, Y)]
+        w3_raw = keep.tile([P, PACK, N], F32, name="w3_raw")
+        slack_rows = [keep.tile([P, S], F32, name="slack_rows%d" % r) for r in range(ROW_TILES)]
+        pos = [[keep.tile([P, S + SPARE], F32, name="pos%d_%d" % (c, r)) for r in range(ROW_TILES)] for c in (X, Y)]
         ident = keep.tile([P, P], F32, name="ident")
 
-        nc.vector.memset(xs[:].bitcast(I32), 0)
-        for q in range(4):
-            nc.scalar.dma_start(out=xs[32 * q:32 * q + 4, :].bitcast(I32), in_=x_scales[0, 4 * q:4 * q + 4, :].bitcast(I32))
-        ws = [w.rearrange("(p j) c -> p j c", j=4) for w in (w1, w2)]
+        nc.gpsimd.memset(table_scales[:].bitcast(I32), 0)
+        w_by_word = [w.rearrange("(p t) i -> p t i", t=PACK) for w in (w1, w2)]
 
-        def load_w(a, r):
-            nc.sync.dma_start(out=w_raw[a][r][:], in_=ws[a][:, :, r * P:(r + 1) * P])
+        def load_weights(r):
+            for c in (X, Y):
+                nc.sync.dma_start(out=w_raw[c][r][:], in_=w_by_word[c][:, :, r * P:(r + 1) * P])
 
-        nc.sync.dma_start(l_offs[:], offs)
-        nc.sync.dma_start(out=xw[:], in_=x_words[0].rearrange("p n t -> p (n t)").bitcast(I32))
-        load_w(0, 0)
-        with nc.allow_non_contiguous_dma(reason="one value a partition"):
-            nc.sync.dma_start(out=un[:], in_=unit.rearrange("(r p) o -> p (r o)", p=P))
-        nc.sync.dma_start(l_req[:], req)
-        load_w(1, 0)
-        nc.sync.dma_start(l_pre[:], pre)
-        nc.sync.dma_start(l_suc[:], suc)
-        for r in range(1, ROWS):
-            load_w(0, r)
-            load_w(1, r)
-            nc.sync.dma_start(out=sl[r - 1][:], in_=slack[(r - 1) * P:r * P, :])
-        nc.sync.dma_start(out=sl[ROWS - 1][:], in_=slack[(ROWS - 1) * P:, :])
-        nc.sync.dma_start(out=w3_raw[:], in_=w3.rearrange("(p j) n -> p j n", j=4))
-        nc.sync.dma_start(out=un4[:], in_=unit.rearrange("(p j) o -> p (j o)", j=4))
+        nc.sync.dma_start(offs_list[:], offs)
+        nc.sync.dma_start(out=table_words[:], in_=x_words[0].rearrange("p n t -> p (n t)").bitcast(I32))
+        for quadrant in range(4):
+            nc.sync.dma_start(out=table_scales[32 * quadrant:32 * quadrant + 4, :].bitcast(I32),
+                              in_=x_scales[0, 4 * quadrant:4 * quadrant + 4, :].bitcast(I32))
+        load_weights(0)
+        with nc.allow_non_contiguous_dma(reason="one value of unit a partition and row tile"):
+            nc.sync.dma_start(out=unit_by_tile[:], in_=unit.rearrange("(r p) o -> p (r o)", p=P))
+        nc.sync.dma_start(req_list[:], req)
+        nc.sync.dma_start(pre_list[:], pre)
+        nc.sync.dma_start(suc_list[:], suc)
+        for r in range(ROW_TILES):
+            if r < LAST:
+                load_weights(r + 1)
+            nc.sync.dma_start(out=slack_rows[r][:], in_=slack[r * P:(r + 1) * P, :])
+        for u in range(2):
+            nc.sync.dma_start(out=w3_raw[:, 2 * u:2 * u + 2, :].rearrange("p e m -> p (e m)"),
+                              in_=w3.rearrange("(b u s e) m -> u b s (e m)", u=2, s=8, e=2)[u])
+            nc.sync.dma_start(out=unit_by_word[u][:], in_=unit.rearrange("(b u s e) o -> u b s (e o)", u=2, s=8, e=2)[u])
 
         make_identity(nc, ident[:])
-        for a in range(2):
-            for r in range(ROWS):
-                nc.gpsimd.memset(pos[a][r][:, S:], 0.0)
+        for c in (X, Y):
+            for r in range(ROW_TILES):
+                nc.gpsimd.memset(pos[c][r][:, S:], 0.0)
 
-        mag = keep.tile([P, ROWS], F32, name="mag")
-        half_mag = keep.tile([P, ROWS], F32, name="half_mag")
-        neg_mag = keep.tile([P, ROWS], F32, name="neg_mag")
-        nc.scalar.activation(out=mag[:], in_=un[:], func=ACT.Abs)
-        nc.scalar.activation(out=half_mag[:], in_=un[:], func=ACT.Abs, scale=0.5)
-        nc.scalar.activation(out=neg_mag[:], in_=mag[:], func=ACT.Copy, scale=-1.0)
+        size = keep.tile([P, ROW_TILES], F32, name="size")
+        half_size = keep.tile([P, ROW_TILES], F32, name="half_size")
+        minus_size = keep.tile([P, ROW_TILES], F32, name="minus_size")
+        nc.scalar.activation(out=size[:], in_=unit_by_tile[:], func=ACT.Abs)
+        nc.scalar.activation(out=half_size[:], in_=unit_by_tile[:], func=ACT.Abs, scale=0.5)
+        nc.scalar.activation(out=minus_size[:], in_=size[:], func=ACT.Copy, scale=-1.0)
 
-        gs = keep.tile([P, S], U8, name="gs", align_bytes=64)
-        gw = keep.tile([P, S], U32, name="gw", align_bytes=64)
-        nc.vector.tensor_copy(gs[:], xs[:].indirect(l_offs[:]))
-        nc.vector.tensor_copy(gw[:], xw[:].bitcast(U32).indirect(l_offs[:]))
+        picked_scales = keep.tile([P, S], U8, name="picked_scales", align_bytes=64)
+        picked_words = keep.tile([P, S], U32, name="picked_words", align_bytes=64)
+        nc.vector.tensor_copy(picked_words[:], table_words[:].bitcast(U32).indirect(offs_list[:]))
+        nc.vector.tensor_copy(picked_scales[:], table_scales[:].indirect(offs_list[:]))
 
-        def position(a, r):
-            raw = w_raw[a][r][:]
-            cast = nc.scalar.copy if r in (0,) else nc.vector.tensor_copy
-            wg = work.tile([P, P, 4], BF16, name="wg", align_bytes=64, bufs=4)
-            cast(out=wg[:].rearrange("p (c i) j -> p c j i", i=4), in_=raw.rearrange("p j (c i) -> p c j i", i=4))
-            wc = work.tile([P, P], U32, name="wc", align_bytes=64, bufs=4)
-            wsc = work.tile([P, P], U8, name="wsc", align_bytes=64, bufs=4)
-            nc.vector.quantize_mx(out=wc[:].bitcast(FP8X4), scales=wsc[:], in_=wg[:].rearrange("p c j -> p (c j)"))
-            acc = psum.tile([P, S], F32, name="acc")
-            nc.tensor.matmul_mx(out=acc[:], lhsT=wc[:].bitcast(FP8X4), lhsT_scale=wsc[:], rhs=gw[:].bitcast(FP8X4), rhs_scale=gs[:], start=True, stop=True)
-            factor = (mag, half_mag)[a][:, r:r + 1]
-            if (a, r) == (1, 0):
-                nc.vector.tensor_scalar(out=pos[a][r][:, :S], in0=acc[:], scalar1=factor, scalar2=None, op0=ALU.mult)
+        def quantise_weights(c, r):
+            round_copy = nc.scalar.copy if r == 0 else nc.vector.tensor_copy
+            grouped = keep.tile([P, P, PACK], BF16, name="grouped%d_%d" % (c, r), align_bytes=64)
+            round_copy(out=grouped[:].rearrange("p (g i) t -> p g t i", i=4),
+                       in_=w_raw[c][r][:].rearrange("p t (g i) -> p g t i", i=4))
+            codes = keep.tile([P, P], U32, name="codes%d_%d" % (c, r), align_bytes=64)
+            scales = keep.tile([P, P], U8, name="scales%d_%d" % (c, r), align_bytes=64)
+            nc.vector.quantize_mx(out=codes[:].bitcast(FP8X4), scales=scales[:], in_=grouped[:].rearrange("p i t -> p (i t)"))
+            return codes, scales
+
+        minus_req = []
+
+        def positions(r, quantised):
+            for c in (X, Y):
+                codes, scales = quantised[c]
+                product = psum.tile([P, S], F32, name="product")
+                nc.tensor.matmul_mx(out=product[:], lhsT=codes[:].bitcast(FP8X4), lhsT_scale=scales[:],
+                                    rhs=picked_words[:].bitcast(FP8X4), rhs_scale=picked_scales[:], start=True, stop=True)
+                factor = (size, half_size)[c][:, r:r + 1]
+                if (c, r) == (Y, 0):
+                    nc.vector.tensor_scalar(out=pos[c][r][:, :S], in0=product[:], scalar1=factor, scalar2=None, op0=ALU.mult)
+                else:
+                    nc.scalar.activation(out=pos[c][r][:, :S], in_=product[:], func=ACT.Copy, scale=factor)
+            fetched = [work.tile([P, S], F32, name="minus_req%d" % c) for c in (X, Y)]
+            for c in (X, Y):
+                nc.scalar.activation(out=fetched[c][:], in_=pos[c][r][:].indirect(req_list[:]), func=ACT.Copy, scale=-1.0)
+            minus_req.append(fetched)
+
+        hid_turned = [keep.tile([P, count // P, H], BF16, name="hid_turned%d" % first) for first, count in PIECES]
+
+        def add_turned(bank, term, count, start, stop):
+            for j in range(0, count, P):
+                nc.tensor.matmul(bank[:, j:j + P].rearrange("p (u b s) -> p b u s", u=2, s=16), lhsT=term[:, j:j + P], rhs=ident[:],
+                                 is_transpose=True, start=start and j == 0, stop=stop and j + P == count)
+
+        def costs(r, first, count):
+            entries = slice(first // STRIPE, (first + count) // STRIPE)
+
+            def fresh(name):
+                return work.tile([P, count], F32, name=name)
+
+            def to_request(c, stops, name, on_scalar):
+                looked_up = pos[c][r][:].indirect(stops[:, entries])
+                if on_scalar:
+                    fetched = fresh(name + "_fetched")
+                    nc.scalar.activation(out=fetched[:], in_=looked_up, func=ACT.Copy)
+                    looked_up = fetched[:]
+                difference = fresh(name)
+                nc.vector.tensor_tensor(difference[:], looked_up, minus_req[r][c][:, first:first + count], ALU.add)
+                return difference
+
+            minus_slack = fresh("minus_slack")
+            if r < SLACK_ON_SCALAR_FROM:
+                nc.vector.tensor_scalar(out=minus_slack[:], in0=slack_rows[r][:, first:first + count],
+                                        scalar1=minus_size[:, r:r + 1], scalar2=None, op0=ALU.mult)
             else:
-                nc.scalar.activation(out=pos[a][r][:, :S], in_=acc[:], func=ACT.Copy, scale=factor)
+                nc.scalar.activation(out=minus_slack[:], in_=slack_rows[r][:, first:first + count], func=ACT.Copy,
+                                     scale=minus_size[:, r:r + 1])
+            over_slack = psum.tile([P, count], F32, name="over_slack")
+            half_ins = psum.tile([P, count], F32, name="half_ins")
+            add_turned(over_slack, minus_slack, count, True, False)
 
-        hid_t = [keep.tile([P, n // P, H], BF16, name="hid_t%d" % j0) for j0, n in GROUPS]
+            def add_distance(difference, name, start, stop):
+                distance = fresh(name)
+                nc.scalar.activation(out=distance[:], in_=difference[:], func=ACT.Abs)
+                add_turned(over_slack, distance, count, False, stop)
+                add_turned(half_ins, distance, count, start, stop)
 
-        def add_turned(bank, term, n, first, last):
-            for c in range(n // P):
-                nc.tensor.matmul(bank[:, c * P:(c + 1) * P], lhsT=term[:, c * P:(c + 1) * P], rhs=ident[:], is_transpose=True,
-                                 start=first and c == 0, stop=last and c == n // P - 1)
+            x_pre = to_request(X, pre_list, "x_pre", False)
+            x_suc = to_request(X, suc_list, "x_suc", False)
+            y_pre = to_request(Y, pre_list, "y_pre", r >= PRE_ON_SCALAR_FROM)
+            add_distance(y_pre, "y_pre_distance", True, False)
+            floored = fresh("floored")
+            nc.vector.scalar_tensor_tensor(out=floored[:], in0=x_pre[:], scalar=0.0, in1=x_suc[:], op0=ALU.min, op1=ALU.max)
+            y_suc = to_request(Y, suc_list, "y_suc", r >= SUC_ON_SCALAR_FROM)
+            add_distance(y_suc, "y_suc_distance", False, False)
+            median = fresh("median")
+            nc.vector.scalar_tensor_tensor(out=median[:], in0=x_pre[:], scalar=0.0, in1=floored[:], op0=ALU.max, op1=ALU.min)
+            add_distance(median, "x_distance", False, True)
 
-        def fetch_req(r, j0, n):
-            cols = slice(j0 // 16, (j0 + n) // 16)
-            nb = work.tile([P, n], F32, name="nb", bufs=3)
-            ne = work.tile([P, n], F32, name="ne", bufs=3)
-            nc.scalar.activation(out=nb[:], in_=pos[0][r][:].indirect(l_req[:, cols]), func=ACT.Copy, scale=-1.0)
-            nc.scalar.activation(out=ne[:], in_=pos[1][r][:].indirect(l_req[:, cols]), func=ACT.Copy, scale=-1.0)
-            return nb[:], ne[:]
-
-        def costs(r, j0, n, nb, ne):
-            cols = slice(j0 // 16, (j0 + n) // 16)
-            px, py = pos[0][r], pos[1][r]
-
-            def fresh(tag):
-                return work.tile([P, n], F32, name=tag)
-
-            ns = fresh("ns")
-            nc.vector.tensor_scalar(out=ns[:], in0=sl[r][:, j0:j0 + n], scalar1=neg_mag[:, r:r + 1], scalar2=None, op0=ALU.mult)
-            u, w, p, q, t, med = fresh("u"), fresh("w"), fresh("p"), fresh("q"), fresh("t"), fresh("med")
-            nc.vector.tensor_tensor(u[:], px[:].indirect(l_pre[:, cols]), nb, ALU.add)
-            nc.vector.tensor_tensor(w[:], px[:].indirect(l_suc[:, cols]), nb, ALU.add)
-            if r in (3,):
-                d = fresh("d")
-                nc.scalar.activation(out=d[:], in_=py[:].indirect(l_pre[:, cols]), func=ACT.Copy)
-                nc.vector.tensor_tensor(p[:], d[:], ne, ALU.add)
-            else:
-                nc.vector.tensor_tensor(p[:], py[:].indirect(l_pre[:, cols]), ne, ALU.add)
-            nc.vector.scalar_tensor_tensor(out=t[:], in0=u[:], scalar=0.0, in1=w[:], op0=ALU.min, op1=ALU.max)
-            if r in (0, 1, 2, 3):
-                f = fresh("f")
-                nc.scalar.activation(out=f[:], in_=py[:].indirect(l_suc[:, cols]), func=ACT.Copy)
-                nc.vector.tensor_tensor(q[:], f[:], ne, ALU.add)
-            else:
-                nc.vector.tensor_tensor(q[:], py[:].indirect(l_suc[:, cols]), ne, ALU.add)
-            nc.vector.scalar_tensor_tensor(out=med[:], in0=u[:], scalar=0.0, in1=t[:], op0=ALU.max, op1=ALU.min)
-            ap, aq, am = fresh("ap"), fresh("aq"), fresh("am")
-            nc.scalar.activation(out=ap[:], in_=p[:], func=ACT.Abs)
-            nc.scalar.activation(out=aq[:], in_=q[:], func=ACT.Abs)
-            nc.scalar.activation(out=am[:], in_=med[:], func=ACT.Abs)
-            over = psum.tile([P, n], F32, name="over")
-            half = psum.tile([P, n], F32, name="half")
-            add_turned(over, ns, n, True, False)
-            add_turned(over, ap, n, False, False)
-            add_turned(half, ap, n, True, False)
-            add_turned(over, aq, n, False, False)
-            add_turned(half, aq, n, False, False)
-            add_turned(over, am, n, False, True)
-            add_turned(half, am, n, False, True)
             late = fresh("late")
-            nc.scalar.activation(out=late[:], in_=over[:], func=ACT.Relu, scale=1.5)
-            for g, (g0, gn) in enumerate(GROUPS):
-                if j0 <= g0 < j0 + n:
-                    part = slice(g0 - j0, g0 - j0 + gn)
+            nc.scalar.activation(out=late[:], in_=over_slack[:], func=ACT.Relu, scale=1.5)
+            for piece, (piece_first, piece_count) in enumerate(PIECES):
+                if first <= piece_first < first + count:
+                    part = slice(piece_first - first, piece_first - first + piece_count)
                     nc.vector.scalar_tensor_tensor(
-                        out=hid_t[g][:, :, r * P:(r + 1) * P],
-                        in0=half[:, part].rearrange("p (c i) -> p c i", i=P), scalar=2.0,
-                        in1=late[:, part].rearrange("p (c i) -> p c i", i=P), op0=ALU.mult, op1=ALU.add)
+                        out=hid_turned[piece][:].rearrange("p g (u r i) -> p (g u) r i", u=2, r=ROW_TILES)[:, :, r, :],
+                        in0=half_ins[:, part].rearrange("p (g i) -> p g i", i=P // 2), scalar=2.0,
+                        in1=late[:, part].rearrange("p (g i) -> p g i", i=P // 2), op0=ALU.mult, op1=ALU.add)
 
-        w3c = keep.tile([P, N], U32, name="w3c", align_bytes=64)
-        w3s = keep.tile([P, N], U8, name="w3s", align_bytes=64)
+        w3_codes = keep.tile([P, N], U32, name="w3_codes", align_bytes=64)
+        w3_scales = keep.tile([P, N], U8, name="w3_scales", align_bytes=64)
 
-        def last_weights():
-            pos_unit = keep.tile([P, 4], F32, name="pos_unit")
-            sign = keep.tile([P, 4], F32, name="sign")
-            nc.vector.tensor_scalar(out=pos_unit[:], in0=un4[:], scalar1=0.0, scalar2=2.0, op0=ALU.is_ge, op1=ALU.mult)
-            nc.vector.tensor_scalar(out=sign[:], in0=pos_unit[:], scalar1=-1.0, scalar2=None, op0=ALU.add)
-            w3g = keep.tile([P, N, 4], BF16, name="w3g", align_bytes=64)
-            nc.vector.tensor_tensor(w3g[:], w3_raw[:].rearrange("p j n -> p n j"), sign[:].unsqueeze(1).to_broadcast([P, N, 4]), ALU.mult)
-            nc.vector.quantize_mx(out=w3c[:].bitcast(FP8X4), scales=w3s[:], in_=w3g[:].rearrange("p n j -> p (n j)"))
+        def quantise_w3():
+            twice_positive = keep.tile([P, PACK], F32, name="twice_positive")
+            sign = keep.tile([P, PACK], F32, name="sign")
+            for u in range(2):
+                nc.gpsimd.tensor_scalar(out=twice_positive[:, 2 * u:2 * u + 2], in0=unit_by_word[u][:], scalar1=0.0, scalar2=2.0,
+                                        op0=ALU.is_ge, op1=ALU.mult)
+            nc.gpsimd.tensor_scalar(out=sign[:], in0=twice_positive[:], scalar1=-1.0, scalar2=None, op0=ALU.add)
+            w3_grouped = keep.tile([P, N, PACK], BF16, name="w3_grouped", align_bytes=64)
+            nc.vector.tensor_tensor(w3_grouped[:], w3_raw[:].rearrange("p t m -> p m t"),
+                                    sign[:].unsqueeze(1).to_broadcast([P, N, PACK]), ALU.mult)
+            nc.vector.quantize_mx(out=w3_codes[:].bitcast(FP8X4), scales=w3_scales[:], in_=w3_grouped[:].rearrange("p m t -> p (m t)"))
 
-        def vehicles(g):
-            j0, n = GROUPS[g]
-            words = hid_t[g][:].rearrange("p c i -> p (c i)").bitcast(F32)
-            back = psum1.tile([P, n // P, 2, P], F32, name="back")
-            for c in range(n // P):
-                for e in range(2):
-                    nc.tensor.transpose(back[:, c, e, :], words[:, c * 256 + e:(c + 1) * 256:2], ident[:])
-            hg = work.tile([P, n * 4], BF16, name="hg", align_bytes=64)
-            nc.scalar.copy(out=hg[:].bitcast(F32).rearrange("p (c j e) -> p c j e", j=P, e=2), in_=back[:].rearrange("p c e j -> p c j e"))
-            hc = work.tile([P, n], U32, name="hc", align_bytes=64)
-            hs = work.tile([P, n], U8, name="hs", align_bytes=64)
-            nc.vector.quantize_mx(out=hc[:].bitcast(FP8X4), scales=hs[:], in_=hg[:])
-            res = psum1.tile([P, n], F32, name="res")
-            nc.tensor.matmul_mx(out=res[:], lhsT=w3c[:].bitcast(FP8X4), lhsT_scale=w3s[:], rhs=hc[:].bitcast(FP8X4), rhs_scale=hs[:], start=True, stop=True)
-            res_sb = work.tile([P, n], F32, name="res_sb")
-            nc.scalar.copy(out=res_sb[:], in_=res[:])
-            nc.sync.dma_start(out=out[:, j0:j0 + n], in_=res_sb[:])
+        def vehicles(piece):
+            first, count = PIECES[piece]
+            pairs = hid_turned[piece][:].rearrange("p g i -> p (g i)").bitcast(F32)
+            turned_back = psum_last.tile([P, count // P, 2, P], F32, name="turned_back")
+            for g in range(count // P):
+                for u in range(2):
+                    nc.tensor.transpose(turned_back[:, g, u, :], pairs[:, (2 * g + u) * P:(2 * g + u + 1) * P], ident[:])
+            hid_grouped = work.tile([P, count * PACK], BF16, name="hid_grouped", align_bytes=64)
+            nc.scalar.copy(out=hid_grouped[:].bitcast(F32).rearrange("p (g j u) -> p g j u", j=P, u=2),
+                           in_=turned_back[:].rearrange("p g u j -> p g j u"))
+            hid_codes = work.tile([P, count], U32, name="hid_codes", align_bytes=64)
+            hid_scales = work.tile([P, count], U8, name="hid_scales", align_bytes=64)
+            nc.vector.quantize_mx(out=hid_codes[:].bitcast(FP8X4), scales=hid_scales[:], in_=hid_grouped[:])
+            result = psum_last.tile([P, count], F32, name="result")
+            nc.tensor.matmul_mx(out=result[:], lhsT=w3_codes[:].bitcast(FP8X4), lhsT_scale=w3_scales[:],
+                                rhs=hid_codes[:].bitcast(FP8X4), rhs_scale=hid_scales[:], start=True, stop=True)
+            staged = work.tile([P, count], F32, name="staged")
+            nc.scalar.copy(out=staged[:], in_=result[:])
+            nc.sync.dma_start(out=out[:, first:first + count], in_=staged[:])
 
-        position(0, 0)
-        position(1, 0)
-        fetched = fetch_req(0, 0, S)
-        for r in range(1, ROWS):
-            position(0, r)
-            position(1, r)
-        for r in range(ROWS - 1):
-            ahead = fetch_req(r + 1, 0, S)
-            costs(r, 0, S, *fetched)
-            fetched = ahead
+        quantised = []
+        for r in range(ROW_TILES):
+            quantised.append([quantise_weights(c, r) for c in (X, Y)])
+            if r < AHEAD:
+                positions(r, quantised[r])
+        for r in range(LAST):
+            costs(r, 0, S)
+            if r + AHEAD < ROW_TILES:
+                positions(r + AHEAD, quantised[r + AHEAD])
             if r == 0:
-                last_weights()
-        for g, (j0, n) in enumerate(GROUPS):
-            costs(ROWS - 1, j0, n, *[f[:, j0:j0 + n] for f in fetched])
-            if g > 0:
-                vehicles(g - 1)
-        vehicles(len(GROUPS) - 1)
+                quantise_w3()
+        for piece, (first, count) in enumerate(PIECES):
+            costs(LAST, first, count)
+            if piece > 0:
+                vehicles(piece - 1)
+        vehicles(len(PIECES) - 1)

@@ -24,9 +24,9 @@ LAST = ROW_TILES - 1
 X, Y = 0, 1
 SPARE = 16
 PIECES = ((0, 256), (256, 128), (384, 128))
-SUC_ON_SCALAR_FROM = 2
-PRE_ON_SCALAR_FROM = 3
-SLACK_ON_SCALAR_FROM = 2
+SUC_ON_SCALAR_FROM = 1
+PRE_ON_SCALAR_FROM = 2
+SLACK_ON_SCALAR_FROM = 3
 AHEAD = 2
 
 

from contextlib import ExitStack

import concourse.mybir as mybir
from concourse.masks import make_identity

K, T, S, N, H = 512, 2048, 512, 128, 512
FLOPS = 2 * (2 * K * H * S) + 2 * H * N * S

F32 = mybir.dt.float32
BF16 = mybir.dt.bfloat16
I32 = mybir.dt.int32
U32 = mybir.dt.uint32
U16 = mybir.dt.uint16
U8 = mybir.dt.uint8
FP8X4 = mybir.dt.float8_e4m3fn_x4
ALU = mybir.AluOpType
ACT = mybir.ActivationFunctionType

P = 128
PACK = 4
STRIPE = 16
ROW_TILES = H // P
LAST = ROW_TILES - 1
X, Y = 0, 1
SPARE = 16
PIECES = ((0, 256), (256, 128), (384, 128))
SUC_ON_SCALAR_FROM = 1
PRE_ON_SCALAR_FROM = 2
SLACK_ON_SCALAR_FROM = 3
AHEAD = 2


def tile_picked_ydarpi_cost_p_kernel(tc, x_words, x_scales, w1, w2, slack, unit, w3, offs, pre, suc, req, out):
    nc = tc.nc
    with ExitStack() as ctx:
        keep = ctx.enter_context(tc.tile_pool(name="keep", bufs=1))
        work = ctx.enter_context(tc.tile_pool(name="work", bufs=3))
        psum = ctx.enter_context(tc.psum_pool(name="psum", bufs=2))
        psum_last = ctx.enter_context(tc.psum_pool(name="psum_last", bufs=1))

        offs_list = keep.tile([P, S // STRIPE], U16, name="offs_list")
        pre_list = keep.tile([P, S // STRIPE], U16, name="pre_list")
        suc_list = keep.tile([P, S // STRIPE], U16, name="suc_list")
        req_list = keep.tile([P, S // STRIPE], U16, name="req_list")
        table_words = keep.tile([P, T], I32, name="table_words")
        table_scales = keep.tile([P, T], U8, name="table_scales")
        unit_by_tile = keep.tile([P, ROW_TILES], F32, name="unit_by_tile")
        unit_by_word = [keep.tile([P, 2], F32, name="unit_by_word%d" % u) for u in range(2)]
        w_raw = [[keep.tile([P, PACK, P], F32, name="w_raw%d_%d" % (c, r)) for r in range(ROW_TILES)] for c in (X, Y)]
        w3_raw = keep.tile([P, PACK, N], F32, name="w3_raw")
        slack_rows = [keep.tile([P, S], F32, name="slack_rows%d" % r) for r in range(ROW_TILES)]
        pos = [[keep.tile([P, S + SPARE], F32, name="pos%d_%d" % (c, r)) for r in range(ROW_TILES)] for c in (X, Y)]
        ident = keep.tile([P, P], F32, name="ident")

        nc.gpsimd.memset(table_scales[:].bitcast(I32), 0)
        w_by_word = [w.rearrange("(p t) i -> p t i", t=PACK) for w in (w1, w2)]

        def load_weights(r):
            for c in (X, Y):
                nc.sync.dma_start(out=w_raw[c][r][:], in_=w_by_word[c][:, :, r * P:(r + 1) * P])

        nc.sync.dma_start(offs_list[:], offs)
        nc.sync.dma_start(out=table_words[:], in_=x_words[0].rearrange("p n t -> p (n t)").bitcast(I32))
        for quadrant in range(4):
            nc.sync.dma_start(out=table_scales[32 * quadrant:32 * quadrant + 4, :].bitcast(I32),
                              in_=x_scales[0, 4 * quadrant:4 * quadrant + 4, :].bitcast(I32))
        load_weights(0)
        with nc.allow_non_contiguous_dma(reason="one value of unit a partition and row tile"):
            nc.sync.dma_start(out=unit_by_tile[:], in_=unit.rearrange("(r p) o -> p (r o)", p=P))
        nc.sync.dma_start(req_list[:], req)
        nc.sync.dma_start(pre_list[:], pre)
        nc.sync.dma_start(suc_list[:], suc)
        for r in range(ROW_TILES):
            if r < LAST:
                load_weights(r + 1)
            nc.sync.dma_start(out=slack_rows[r][:], in_=slack[r * P:(r + 1) * P, :])
        for u in range(2):
            nc.sync.dma_start(out=w3_raw[:, 2 * u:2 * u + 2, :].rearrange("p e m -> p (e m)"),
                              in_=w3.rearrange("(b u s e) m -> u b s (e m)", u=2, s=8, e=2)[u])
            nc.sync.dma_start(out=unit_by_word[u][:], in_=unit.rearrange("(b u s e) o -> u b s (e o)", u=2, s=8, e=2)[u])

        make_identity(nc, ident[:])
        for c in (X, Y):
            for r in range(ROW_TILES):
                nc.gpsimd.memset(pos[c][r][:, S:], 0.0)

        size = keep.tile([P, ROW_TILES], F32, name="size")
        half_size = keep.tile([P, ROW_TILES], F32, name="half_size")
        minus_size = keep.tile([P, ROW_TILES], F32, name="minus_size")
        nc.scalar.activation(out=size[:], in_=unit_by_tile[:], func=ACT.Abs)
        nc.scalar.activation(out=half_size[:], in_=unit_by_tile[:], func=ACT.Abs, scale=0.5)
        nc.scalar.activation(out=minus_size[:], in_=size[:], func=ACT.Copy, scale=-1.0)

        picked_scales = keep.tile([P, S], U8, name="picked_scales", align_bytes=64)
        picked_words = keep.tile([P, S], U32, name="picked_words", align_bytes=64)
        nc.vector.tensor_copy(picked_words[:], table_words[:].bitcast(U32).indirect(offs_list[:]))
        nc.vector.tensor_copy(picked_scales[:], table_scales[:].indirect(offs_list[:]))

        def quantise_weights(c, r):
            round_copy = nc.scalar.copy if r == 0 else nc.vector.tensor_copy
            grouped = keep.tile([P, P, PACK], BF16, name="grouped%d_%d" % (c, r), align_bytes=64)
            round_copy(out=grouped[:].rearrange("p (g i) t -> p g t i", i=4),
                       in_=w_raw[c][r][:].rearrange("p t (g i) -> p g t i", i=4))
            codes = keep.tile([P, P], U32, name="codes%d_%d" % (c, r), align_bytes=64)
            scales = keep.tile([P, P], U8, name="scales%d_%d" % (c, r), align_bytes=64)
            nc.vector.quantize_mx(out=codes[:].bitcast(FP8X4), scales=scales[:], in_=grouped[:].rearrange("p i t -> p (i t)"))
            return codes, scales

        minus_req = []

        def positions(r, quantised):
            for c in (X, Y):
                codes, scales = quantised[c]
                product = psum.tile([P, S], F32, name="product")
                nc.tensor.matmul_mx(out=product[:], lhsT=codes[:].bitcast(FP8X4), lhsT_scale=scales[:],
                                    rhs=picked_words[:].bitcast(FP8X4), rhs_scale=picked_scales[:], start=True, stop=True)
                factor = (size, half_size)[c][:, r:r + 1]
                if (c, r) == (Y, 0):
                    nc.vector.tensor_scalar(out=pos[c][r][:, :S], in0=product[:], scalar1=factor, scalar2=None, op0=ALU.mult)
                else:
                    nc.scalar.activation(out=pos[c][r][:, :S], in_=product[:], func=ACT.Copy, scale=factor)
            fetched = [work.tile([P, S], F32, name="minus_req%d" % c) for c in (X, Y)]
            for c in (X, Y):
                nc.scalar.activation(out=fetched[c][:], in_=pos[c][r][:].indirect(req_list[:]), func=ACT.Copy, scale=-1.0)
            minus_req.append(fetched)

        hid_turned = [keep.tile([P, count // P, H], BF16, name="hid_turned%d" % first) for first, count in PIECES]

        def add_turned(bank, term, count, start, stop):
            for j in range(0, count, P):
                nc.tensor.matmul(bank[:, j:j + P].rearrange("p (u b s) -> p b u s", u=2, s=16), lhsT=term[:, j:j + P], rhs=ident[:],
                                 is_transpose=True, start=start and j == 0, stop=stop and j + P == count)

        def costs(r, first, count):
            entries = slice(first // STRIPE, (first + count) // STRIPE)

            def fresh(name):
                return work.tile([P, count], F32, name=name)

            def to_request(c, stops, name, on_scalar):
                looked_up = pos[c][r][:].indirect(stops[:, entries])
                if on_scalar:
                    fetched = fresh(name + "_fetched")
                    nc.scalar.activation(out=fetched[:], in_=looked_up, func=ACT.Copy)
                    looked_up = fetched[:]
                difference = fresh(name)
                nc.vector.tensor_tensor(difference[:], looked_up, minus_req[r][c][:, first:first + count], ALU.add)
                return difference

            minus_slack = fresh("minus_slack")
            if r < SLACK_ON_SCALAR_FROM:
                nc.vector.tensor_scalar(out=minus_slack[:], in0=slack_rows[r][:, first:first + count],
                                        scalar1=minus_size[:, r:r + 1], scalar2=None, op0=ALU.mult)
            else:
                nc.scalar.activation(out=minus_slack[:], in_=slack_rows[r][:, first:first + count], func=ACT.Copy,
                                     scale=minus_size[:, r:r + 1])
            over_slack = psum.tile([P, count], F32, name="over_slack")
            half_ins = psum.tile([P, count], F32, name="half_ins")
            add_turned(over_slack, minus_slack, count, True, False)

            def add_distance(difference, name, start, stop):
                distance = fresh(name)
                nc.scalar.activation(out=distance[:], in_=difference[:], func=ACT.Abs)
                add_turned(over_slack, distance, count, False, stop)
                add_turned(half_ins, distance, count, start, stop)

            x_pre = to_request(X, pre_list, "x_pre", False)
            x_suc = to_request(X, suc_list, "x_suc", False)
            y_pre = to_request(Y, pre_list, "y_pre", r >= PRE_ON_SCALAR_FROM)
            add_distance(y_pre, "y_pre_distance", True, False)
            floored = fresh("floored")
            nc.vector.scalar_tensor_tensor(out=floored[:], in0=x_pre[:], scalar=0.0, in1=x_suc[:], op0=ALU.min, op1=ALU.max)
            y_suc = to_request(Y, suc_list, "y_suc", r >= SUC_ON_SCALAR_FROM)
            add_distance(y_suc, "y_suc_distance", False, False)
            median = fresh("median")
            nc.vector.scalar_tensor_tensor(out=median[:], in0=x_pre[:], scalar=0.0, in1=floored[:], op0=ALU.max, op1=ALU.min)
            add_distance(median, "x_distance", False, True)

            late = fresh("late")
            nc.scalar.activation(out=late[:], in_=over_slack[:], func=ACT.Relu, scale=1.5)
            for piece, (piece_first, piece_count) in enumerate(PIECES):
                if first <= piece_first < first + count:
                    part = slice(piece_first - first, piece_first - first + piece_count)
                    nc.vector.scalar_tensor_tensor(
                        out=hid_turned[piece][:].rearrange("p g (u r i) -> p (g u) r i", u=2, r=ROW_TILES)[:, :, r, :],
                        in0=half_ins[:, part].rearrange("p (g i) -> p g i", i=P // 2), scalar=2.0,
                        in1=late[:, part].rearrange("p (g i) -> p g i", i=P // 2), op0=ALU.mult, op1=ALU.add)

        w3_codes = keep.tile([P, N], U32, name="w3_codes", align_bytes=64)
        w3_scales = keep.tile([P, N], U8, name="w3_scales", align_bytes=64)

        def quantise_w3():
            twice_positive = keep.tile([P, PACK], F32, name="twice_positive")
            sign = keep.tile([P, PACK], F32, name="sign")
            for u in range(2):
                nc.gpsimd.tensor_scalar(out=twice_positive[:, 2 * u:2 * u + 2], in0=unit_by_word[u][:], scalar1=0.0, scalar2=2.0,
                                        op0=ALU.is_ge, op1=ALU.mult)
            nc.gpsimd.tensor_scalar(out=sign[:], in0=twice_positive[:], scalar1=-1.0, scalar2=None, op0=ALU.add)
            w3_grouped = keep.tile([P, N, PACK], BF16, name="w3_grouped", align_bytes=64)
            nc.vector.tensor_tensor(w3_grouped[:], w3_raw[:].rearrange("p t m -> p m t"),
                                    sign[:].unsqueeze(1).to_broadcast([P, N, PACK]), ALU.mult)
            nc.vector.quantize_mx(out=w3_codes[:].bitcast(FP8X4), scales=w3_scales[:], in_=w3_grouped[:].rearrange("p m t -> p (m t)"))

        def vehicles(piece):
            first, count = PIECES[piece]
            pairs = hid_turned[piece][:].rearrange("p g i -> p (g i)").bitcast(F32)
            turned_back = psum_last.tile([P, count // P, 2, P], F32, name="turned_back")
            for g in range(count // P):
                for u in range(2):
                    nc.tensor.transpose(turned_back[:, g, u, :], pairs[:, (2 * g + u) * P:(2 * g + u + 1) * P], ident[:])
            hid_grouped = work.tile([P, count * PACK], BF16, name="hid_grouped", align_bytes=64)
            nc.scalar.copy(out=hid_grouped[:].bitcast(F32).rearrange("p (g j u) -> p g j u", j=P, u=2),
                           in_=turned_back[:].rearrange("p g u j -> p g j u"))
            hid_codes = work.tile([P, count], U32, name="hid_codes", align_bytes=64)
            hid_scales = work.tile([P, count], U8, name="hid_scales", align_bytes=64)
            nc.vector.quantize_mx(out=hid_codes[:].bitcast(FP8X4), scales=hid_scales[:], in_=hid_grouped[:])
            result = psum_last.tile([P, count], F32, name="result")
            nc.tensor.matmul_mx(out=result[:], lhsT=w3_codes[:].bitcast(FP8X4), lhsT_scale=w3_scales[:],
                                rhs=hid_codes[:].bitcast(FP8X4), rhs_scale=hid_scales[:], start=True, stop=True)
            staged = work.tile([P, count], F32, name="staged")
            nc.scalar.copy(out=staged[:], in_=result[:])
            nc.sync.dma_start(out=out[:, first:first + count], in_=staged[:])

        quantised = []
        for r in range(ROW_TILES):
            quantised.append([quantise_weights(c, r) for c in (X, Y)])
            if r < AHEAD:
                positions(r, quantised[r])
        for r in range(LAST):
            costs(r, 0, S)
            if r + AHEAD < ROW_TILES:
                positions(r + AHEAD, quantised[r + AHEAD])
            if r == 0:
                quantise_w3()
        for piece, (first, count) in enumerate(PIECES):
            costs(LAST, first, count)
            if piece > 0:
                vehicles(piece - 1)
        vehicles(len(PIECES) - 1)
